import numpy as np
import ml_dtypes


def mxq(x, axis, fmt="e4m3"):
    dtype, down = {"e4m3": (ml_dtypes.float8_e4m3fn, 7), "e5m2": (ml_dtypes.float8_e5m2, 14)}[fmt]
    v = np.moveaxis(np.asarray(x, np.float32).astype(ml_dtypes.bfloat16).astype(np.float64), axis, -1)
    blocks = v.reshape(v.shape[:-1] + (-1, 32))
    amax = np.abs(blocks).max(-1, keepdims=True)
    byte = np.maximum(np.where(amax > 0, np.frexp(amax)[1] - 1 + 127, 0) - down, 1)
    scale = np.exp2(byte - 127.0)
    codes = (blocks / scale).astype(np.float32).astype(dtype).astype(np.float64)
    return np.moveaxis((codes * scale).reshape(v.shape), -1, axis)


WIDE = False


def mx_kscale(k):
    if not WIDE:
        return np.ones(k)
    levels = np.array([10, -10, 5, -5, 0])
    if k % 512:
        return np.exp2(np.random.permutation(np.resize(levels, k // 32))).repeat(32)
    a = np.empty((k // 512, 16))
    for p in range(k // 512):
        a[p, :8] = np.random.permutation(np.resize(levels, 8))
        for g in range(8):
            far = levels[np.abs(levels - a[p, g]) >= 10]
            a[p, g + 8] = far[np.random.randint(len(far))]
    return np.exp2(a.ravel()).repeat(32)


BF16 = ml_dtypes.bfloat16


def bf(x):
    return np.asarray(x, np.float32).astype(BF16)


def f64(x):
    return np.asarray(x).astype(np.float64)


E2M1 = np.array([0.0, 0.5, 1.0, 1.5, 2.0, 3.0, 4.0, 6.0, -0.0, -0.5, -1.0, -1.5, -2.0, -3.0, -4.0, -6.0])


def pack_weight(w, fmt):
    k, n = w.shape
    w = f64(bf(w)).reshape(k // 32, 32, n)
    amax = np.abs(w).max(1)
    if fmt == "e4m3":
        byte = np.frexp(amax)[1] - 1 + 127 - 7
    else:
        mant, ex = np.frexp(amax / 6.0)
        byte = np.where(mant > 0.5, ex, ex - 1) + 127
    byte = np.clip(np.where(amax > 0, byte, 1), 1, 254)
    scaled = (w * np.exp2(127.0 - byte)[:, None, :]).reshape(k, n).astype(np.float32)
    by_word = np.ascontiguousarray(scaled.reshape(k // 512, 128, 4, n).transpose(0, 1, 3, 2))
    if fmt == "e4m3":
        words = by_word.astype(ml_dtypes.float8_e4m3fn).view(np.uint8)
    else:
        c = by_word.astype(ml_dtypes.float4_e2m1fn).view(np.uint8) & 0xF
        words = c[..., 0::2] | (c[..., 1::2] << 4)
    return np.ascontiguousarray(words), np.ascontiguousarray(byte.astype(np.uint8).reshape(k // 512, 16, n))


def unpack_weight(words, scales, fmt):
    g, p, n, _ = words.shape
    if fmt == "e4m3":
        vals = np.ascontiguousarray(words).view(ml_dtypes.float8_e4m3fn).astype(np.float64)
    else:
        nib = np.empty((g, p, n, 4), np.uint8)
        nib[..., 0::2] = words & 0xF
        nib[..., 1::2] = words >> 4
        vals = E2M1[nib]
    vals = vals * np.repeat(np.exp2(scales.astype(np.float64) - 127.0), 8, axis=1)[..., None]
    return vals.transpose(0, 1, 3, 2).reshape(g * 512, n)
def pack4(w):
    words, scales = pack_weight(w, "e2m1")
    return words.reshape(words.shape[0], 128, -1), scales


def unpack4(words, scales):
    return unpack_weight(words.reshape(words.shape[0], 128, -1, 2), scales, "e2m1")


E4M3FN = np.array([(-1.0 if i & 128 else 1.0) * ((1.0 + (i & 7) / 8.0) * 2.0 ** (((i >> 3) & 15) - 7) if i & 120 else (i & 7) * 2.0 ** -9) for i in range(256)])


def e4m3fn_bytes(y):
    return np.clip(np.asarray(y, np.float64), -448.0, 448.0).astype(np.float32).astype(ml_dtypes.float8_e4m3fn).view(np.uint8)


def e4m3fn_values(b):
    return E4M3FN[b]


N, X, P, M, E, C, H = 1024, 3, 3, 512, 2, 512, 512
WIDTH2 = 0.0018


def plane_coords(pts):
    u = np.stack([pts[:, 0], pts[:, 0], pts[:, 1]], axis=0)
    v = np.stack([pts[:, 1], pts[:, 2], pts[:, 2]], axis=0)
    return u, v


def softmax_last(s):
    e = np.exp(s - np.max(s, axis=-1, keepdims=True))
    return e / np.sum(e, axis=-1, keepdims=True)


def softplus(t):
    return np.maximum(t, 0.0) + np.log(1.0 + np.exp(-np.abs(t)))


def draw0():
    sm, sc = mx_kscale(M), mx_kscale(C)
    pts = bf(np.random.uniform(0.0, 1.0, (N, X)))
    cen = bf(np.random.uniform(0.0, 1.0, (P, M, E)))
    ga = bf(np.random.standard_normal((P, M)) * sm)
    feat = bf(np.random.standard_normal((P, M, C)) * 0.106 * np.sqrt(M) / sm[None, :, None])
    gc = bf((1.0 + 0.1 * np.random.standard_normal(C)) * sc)
    w1_words, w1_scales = pack4(np.random.standard_normal((C, H)) * 2.0 / np.sqrt(C) / sc[:, None])
    b1 = bf(np.random.standard_normal(H) * 0.4)
    return {
        "pts": pts,
        "cen": cen,
        "ga": ga,
        "feat": feat,
        "gc": gc,
        "w1_words": w1_words,
        "w1_scales": w1_scales,
        "b1": b1,
    }


def core(pts, cen, ga, feat, gc, w1_words, w1_scales, b1):
    pts, cen, ga, feat, gc, b1 = f64(pts), f64(cen), f64(ga), f64(feat), f64(gc), f64(b1)
    u, v = plane_coords(pts)
    du = u[:, :, None] - cen[:, None, :, 0]
    dv = v[:, :, None] - cen[:, None, :, 1]
    d2 = du * du + dv * dv
    k = softmax_last(-d2 / WIDTH2)
    a = k * ga[:, None, :]
    f = mxq(a, 2, "e4m3") @ mxq(feat, 1, "e4m3")
    z = f[0] * f[1] * f[2] * gc[None, :]
    t = (mxq(z, 1, "e4m3") @ unpack4(w1_words, w1_scales)) + b1[None, :]
    return softplus(t)


def setup_inputs():
    drawn = draw0()
    full = np.asarray(drawn['feat']).astype(np.float64)
    scale = (np.abs(full).reshape(3, 4, 128, 4, 128).max(axis=(2, 4)) / 448.0).astype(np.float32)
    given = {}
    for key, value in drawn.items():
        if key == 'feat':
            given['feat_bytes'] = e4m3fn_bytes(full / np.repeat(np.repeat(scale.astype(np.float64), 128, axis=1), 128, axis=2))
            given['feat_scale'] = scale
        else:
            given[key] = value
    return given


def reference(pts, cen, ga, feat_bytes, feat_scale, gc, w1_words, w1_scales, b1):
    return core(pts, cen, ga, e4m3fn_values(feat_bytes) * np.repeat(np.repeat(feat_scale.astype(np.float64), 128, axis=1), 128, axis=2), gc, w1_words, w1_scales, b1)

@@ -1,0 +1,367 @@
+from contextlib import ExitStack
+
+import concourse.mybir as mybir
+from concourse.masks import make_identity
+
+N, PLANES, M, C, H = 1024, 3, 512, 512, 512
+INV_WIDTH2 = 1.0 / 0.0018
+COORDS = ((0, 1), (0, 2), (1, 2))
+
+P = 128
+T = 4
+NT = N // P
+UNITS = NT * PLANES
+
+FLOPS = 2 * N * M * C * PLANES + 2 * N * C * H
+
+F32 = mybir.dt.float32
+BF16 = mybir.dt.bfloat16
+U32 = mybir.dt.uint32
+I32 = mybir.dt.int32
+U8 = mybir.dt.uint8
+FP8 = mybir.dt.float8_e4m3fn
+FP8X4 = mybir.dt.float8_e4m3fn_x4
+FP4X4 = mybir.dt.float4_e2m1fn_x4
+ALU = mybir.AluOpType
+ACT = mybir.ActivationFunctionType
+
+BLOCKS = ((0, 256), (256, 256), (512, 256), (768, 256))
+ORDER = (
+    ("CP", 6),
+    ("F", 8),
+    ("EX", 2),
+    ("ST", 5),
+    ("CL", 14),
+    ("O", 9),
+    ("P1", 0),
+    ("W", 5),
+    ("E", 15),
+    ("Z", 8),
+    ("TB", 9),
+    ("Q", 6),
+    ("RC", 2),
+    ("SQ", 0),
+    ("QZ", 8),
+    ("T", -1),
+)
+FEAT = ((-5, "W", 2), (2, "W", 1), (3, "W", 0), (7, "Q", 0), (7, "Q", 1), (8, "Q", 2))
+CP_ON_VECTOR = (0, 1, 22, 23)
+C0_ON_SCALAR = (4, 5, 6)
+LN_EARLY = ((0, 2), (2, 4), (4, 6))
+LN_LATE = ((6, 7), (7, 8))
+SQ_PACE = (2, 6, 4)
+
+
+def tile_kplanesgaussiananchordecoder_d2p_kernel(
+    tc, pts, cen, ga, feat_bytes, feat_scale, gc, w1_words, w1_scales, b1, out
+):
+    nc = tc.nc
+    with ExitStack() as ctx:
+        keep = ctx.enter_context(tc.tile_pool(name="keep", bufs=1))
+        prep = ctx.enter_context(tc.tile_pool(name="prep", bufs=3))
+        sqp = ctx.enter_context(tc.tile_pool(name="sqp", bufs=5))
+        work = ctx.enter_context(tc.tile_pool(name="work", bufs=4))
+        psum = ctx.enter_context(tc.psum_pool(name="psum", bufs=2))
+
+        ptsb = keep.tile([P, N, 3], BF16, name="ptsb")
+        cenb = keep.tile([P, PLANES, 2 * T], BF16, name="cenb")
+        gab = keep.tile([P, PLANES, M], BF16, name="gab")
+        b1b = keep.tile([P, H], BF16, name="b1b")
+        gcb = keep.tile([P, T], BF16, name="gcb")
+        fscale = keep.tile([P, PLANES, 4], F32, name="fscale")
+        w1w = keep.tile([P, 2 * H], U8, name="w1w", align_bytes=64)
+        w1s = keep.tile([P, H], U8, name="w1s", align_bytes=64)
+        fbytes = [keep.tile([P, T, C], U8, name="fbytes%d" % a) for a in range(PLANES)]
+
+        flat = pts.rearrange("n x -> (n x)")
+        n_first = BLOCKS[0][1]
+        nc.scalar.dma_start(out=cenb[:], in_=cen.rearrange("a (p k) e -> p a (k e)", k=T))
+        nc.sync.dma_start(
+            out=ptsb[:, 0:n_first, :].rearrange("p n x -> p (n x)"),
+            in_=flat[0 : 3 * n_first].partition_broadcast(P),
+        )
+        nc.sync.dma_start(out=fbytes[0][:], in_=feat_bytes[0].rearrange("(p t) c -> p t c", t=T))
+        for i in range(4):
+            nc.sync.dma_start(
+                out=fscale[32 * i : 32 * i + 32, :, :],
+                in_=feat_scale.rearrange("a i j -> i a j")[i].partition_broadcast(32),
+            )
+        nc.sync.dma_start(
+            out=ptsb[:, n_first:N, :].rearrange("p n x -> p (n x)"),
+            in_=flat[3 * n_first : 3 * N].partition_broadcast(P),
+        )
+        nc.sync.dma_start(out=gab[:].rearrange("p a m -> p (a m)"), in_=ga.rearrange("a m -> (a m)").partition_broadcast(P))
+        for a in (1, 2):
+            nc.sync.dma_start(out=fbytes[a][:], in_=feat_bytes[a].rearrange("(p t) c -> p t c", t=T))
+        nc.sync.dma_start(out=gcb[:], in_=gc.rearrange("(p t) -> p t", t=T))
+        nc.sync.dma_start(out=b1b[:], in_=b1.partition_broadcast(P))
+        nc.sync.dma_start(out=w1w[:].bitcast(I32), in_=w1_words[0].bitcast(I32))
+        nc.gpsimd.memset(w1s[:].bitcast(I32), 0)
+        for q in range(4):
+            nc.sync.dma_start(
+                out=w1s[32 * q : 32 * q + 4, :].bitcast(I32), in_=w1_scales[0][4 * q : 4 * q + 4, :].bitcast(I32)
+            )
+
+        ident = keep.tile([P, P], F32, name="ident")
+        make_identity(nc, ident[:])
+        cen32 = keep.tile([P, PLANES, 2 * T], F32, name="cen32")
+        nc.vector.tensor_copy(out=cen32[:], in_=cenb[:])
+        gc32 = keep.tile([P, T], F32, name="gc32")
+        gar = keep.tile([P, PLANES, M], BF16, name="gar")
+        fcodes = [keep.tile([P, C], U32, name="fcodes%d" % a, align_bytes=64) for a in range(PLANES)]
+        fplane = [keep.tile([P, C], U8, name="fplane%d" % a, align_bytes=64) for a in range(PLANES)]
+        t_all = keep.tile([P, NT, H], F32, name="t_all")
+        e_all = keep.tile([P, NT, H], F32, name="e_all")
+
+        nc.gpsimd.tensor_copy(out=gc32[:], in_=gcb[:])
+        sqs, d2s, xs, mns, exs, sms, rss, abs_, ats, grs, cos, fs, gs = {}, {}, {}, {}, {}, {}, {}, {}, {}, {}, {}, {}, {}
+        zcs, os_, lows, fgs = {}, {}, {}, {}
+
+        def feat_widen(a):
+            wide = prep.tile([P, T, C], BF16, name="wide")
+            nc.vector.tensor_copy(
+                out=wide[:].rearrange("p t c -> p (t c)"),
+                in_=fbytes[a][:].rearrange("p t c -> p (t c)").bitcast(FP8),
+            )
+            fgrouped = prep.tile([P, T, P, T], BF16, name="fgrouped", align_bytes=64)
+            for j in range(4):
+                cols = slice(32 * j, 32 * j + 32)
+                nc.gpsimd.tensor_scalar(
+                    out=fgrouped[:, :, cols, :],
+                    in0=wide[:, :, 128 * j : 128 * j + 128].rearrange("p t (c s) -> p s c t", s=T),
+                    scalar1=fscale[:, a, j : j + 1],
+                    scalar2=0.0,
+                    op0=ALU.mult,
+                    op1=ALU.add,
+                )
+            nc.gpsimd.tensor_copy(
+                out=gar[:, a, :].rearrange("p (u q e) -> p u q e", u=2, e=2),
+                in_=gab[:, a, :].rearrange("p (q u e) -> p u q e", u=2, e=2),
+            )
+            fgs[a] = fgrouped
+
+        def feat_quantise(a):
+            nc.vector.quantize_mx(
+                out=fcodes[a][:].bitcast(FP8X4), scales=fplane[a][:], in_=fgs[a][:].rearrange("p s c t -> p (s c t)")
+            )
+
+        pieces = [(b, a, t, e) for b in range(len(BLOCKS)) for a in range(PLANES) for t in range(T) for e in range(2)]
+
+        def square(b, a, t, e):
+            n0, width = BLOCKS[b]
+            if (b, a) not in sqs:
+                sq = sqp.tile([P, T, 2, width], F32, name="sq")
+                sqs[(b, a)] = sq
+            nc.scalar.activation(
+                out=sqs[(b, a)][:, t, e, :],
+                in_=ptsb[:, n0 : n0 + width, COORDS[a][e]],
+                func=ACT.Square,
+                bias=cen32[:, a, 2 * t + e : 2 * t + e + 1],
+                scale=-1.0,
+            )
+
+        def block_of(j):
+            return [b for b, (n0, width) in enumerate(BLOCKS) if n0 <= P * j < n0 + width][0]
+
+        def squares_until(count):
+            while len(pieces) > len(BLOCKS) * 24 - count:
+                square(*pieces[0])
+                pieces.remove(pieces[0])
+
+        def squares_next(count):
+            squares_until(min(len(BLOCKS) * 24, len(BLOCKS) * 24 - len(pieces) + count))
+
+        def T_(u):
+            j, a = divmod(u, PLANES)
+            b = block_of(j)
+            squares_until(24 * b + 8 * a + 8)
+            col0 = P * j - BLOCKS[b][0]
+            d2 = psum.tile([P, M], F32, name="d2", bufs=2)
+            for t in range(T):
+                pos = (t % 2) * 256 + (t // 2) * 128
+                for e in range(2):
+                    nc.tensor.matmul(
+                        out=d2[:, pos : pos + P],
+                        lhsT=sqs[(b, a)][:, t, e, col0 : col0 + P],
+                        rhs=ident[:],
+                        start=(e == 0),
+                        stop=(e == 1),
+                        is_transpose=True,
+                    )
+            d2s[u] = d2
+
+        def P1_(u):
+            j, a = divmod(u, PLANES)
+            x = work.tile([P, M], F32, name="x")
+            mn = work.tile([P, 1], F32, name="mn")
+            nc.vector.tensor_scalar(
+                out=x[:], in0=d2s[u][:], scalar1=INV_WIDTH2, scalar2=None, op0=ALU.mult, op1=ALU.min, accum_out=mn[:]
+            )
+            xs[u], mns[u] = x, mn
+
+        def EX_(u):
+            j, a = divmod(u, PLANES)
+            if a == 0:
+                sm = work.tile([P, PLANES], F32, name="sm")
+                sms[j] = sm
+            ex = work.tile([P, M], F32, name="ex", bufs=8)
+            nc.scalar.activation(
+                out=ex[:].rearrange("n (w e) -> n w e", e=2),
+                in_=xs[u][:].rearrange("n (e w) -> n w e", e=2),
+                func=ACT.Exp,
+                bias=mns[u][:],
+                scale=-1.0,
+                accum_out=sms[j][:, a : a + 1],
+            )
+            exs[u] = ex
+
+        def RC_(u):
+            j, a = divmod(u, PLANES)
+            if a == PLANES - 1:
+                rs = work.tile([P, PLANES], F32, name="rs")
+                nc.vector.reciprocal(out=rs[:], in_=sms[j][:])
+                rss[j] = rs
+
+        def ST_(u):
+            j, a = divmod(u, PLANES)
+            ab = work.tile([P, M], BF16, name="ab")
+            nc.vector.scalar_tensor_tensor(
+                out=ab[:], in0=exs[u][:], scalar=rss[j][:, a : a + 1], in1=gar[:, a, :], op0=ALU.mult, op1=ALU.mult
+            )
+            abs_[u] = ab
+
+        def W_(u):
+            at = psum.tile([P, 2, P], F32, name="at", bufs=2)
+            words = abs_[u][:].bitcast(F32)
+            for i in range(2):
+                nc.tensor.transpose(at[:, i, :], words[:, P * i : P * i + P], ident[:])
+            ats[u] = at
+
+        def CP_(u):
+            grouped = work.tile([P, P, T], BF16, name="grouped", align_bytes=64)
+            copy = nc.vector.tensor_copy if u in CP_ON_VECTOR else nc.scalar.copy
+            copy(
+                out=grouped[:].rearrange("p n t -> p (n t)").bitcast(F32).rearrange("p (n u) -> p n u", u=2),
+                in_=ats[u][:].rearrange("p u n -> p n u"),
+            )
+            grs[u] = grouped
+
+        def Q_(u):
+            codes = work.tile([P, P], U32, name="codes", bufs=6, align_bytes=64)
+            plane = work.tile([P, P], U8, name="plane", bufs=6, align_bytes=64)
+            nc.vector.quantize_mx(
+                out=codes[:].bitcast(FP8X4), scales=plane[:], in_=grs[u][:].rearrange("p n t -> p (n t)")
+            )
+            cos[u] = (codes, plane)
+
+        def F_(u):
+            j, a = divmod(u, PLANES)
+            f = psum.tile([P, T, P], F32, name="f", bufs=3)
+            codes, plane = cos[u]
+            for s in range(T):
+                cols = slice(P * s, P * s + P)
+                nc.tensor.matmul_mx(
+                    out=f[:, s, :],
+                    lhsT=fcodes[a][:, cols].bitcast(FP8X4),
+                    lhsT_scale=fplane[a][:, cols],
+                    rhs=codes[:].bitcast(FP8X4),
+                    rhs_scale=plane[:],
+                    start=True,
+                    stop=True,
+                )
+            fs[u] = f
+
+        def Z_(u):
+            j, a = divmod(u, PLANES)
+            if a < PLANES - 1:
+                g = work.tile([P, T, P], F32, name="g")
+                if a == 0 and j in C0_ON_SCALAR:
+                    for s in range(T):
+                        nc.scalar.activation(out=g[:, s, :], in_=fs[u][:, s, :], func=ACT.Copy, scale=gc32[:, s : s + 1])
+                elif a == 0:
+                    nc.vector.tensor_tensor(
+                        out=g[:], in0=fs[u][:], in1=gc32[:].unsqueeze(2).to_broadcast([P, T, P]), op=ALU.mult
+                    )
+                else:
+                    nc.vector.tensor_tensor(out=g[:], in0=fs[u][:], in1=gs[u - 1][:], op=ALU.mult)
+            else:
+                g = work.tile([P, P, T], BF16, name="z", align_bytes=64)
+                nc.vector.tensor_tensor(
+                    out=g[:],
+                    in0=fs[u][:].rearrange("p s n -> p n s"),
+                    in1=gs[u - 1][:].rearrange("p s n -> p n s"),
+                    op=ALU.mult,
+                )
+            gs[u] = g
+
+        def QZ_(j):
+            zcodes = work.tile([P, P], U32, name="zcodes", align_bytes=64)
+            zplane = work.tile([P, P], U8, name="zplane", align_bytes=64)
+            nc.vector.quantize_mx(
+                out=zcodes[:].bitcast(FP8X4), scales=zplane[:], in_=gs[3 * j + 2][:].rearrange("p n t -> p (n t)")
+            )
+            zcs[j] = (zcodes, zplane)
+
+        def O_(j):
+            o = psum.tile([P, H], F32, name="o", bufs=1)
+            zcodes, zplane = zcs[j]
+            nc.tensor.matmul_mx(
+                out=o[:],
+                lhsT=zcodes[:].bitcast(FP8X4),
+                lhsT_scale=zplane[:],
+                rhs=w1w[:].bitcast(FP4X4),
+                rhs_scale=w1s[:],
+                start=True,
+                stop=True,
+            )
+            os_[j] = o
+
+        def TB_(j):
+            nc.vector.tensor_tensor(out=t_all[:, j, :], in0=os_[j][:], in1=b1b[:], op=ALU.add)
+
+        def CL_(j):
+            low = work.tile([P, H], F32, name="low")
+            nc.gpsimd.tensor_scalar(
+                out=low[:], in0=t_all[:, j, :], scalar1=40.0, scalar2=-100.0, op0=ALU.min, op1=ALU.max
+            )
+            lows[j] = low
+
+        def E_(j):
+            nc.scalar.activation(out=e_all[:, j, :], in_=lows[j][:], func=ACT.Exp)
+            if j == LN_EARLY[-1][1] - 1:
+                logs(LN_EARLY)
+
+        def logs(groups):
+            for j0, j1 in groups:
+                nc.scalar.activation(out=e_all[:, j0:j1, :], in_=e_all[:, j0:j1, :], func=ACT.Ln, bias=1.0)
+
+        out_view = out.rearrange("(j n) h -> n j h", n=P)
+
+        def finish(groups):
+            for j0, j1 in groups:
+                nc.vector.tensor_tensor(out=t_all[:, j0:j1, :], in0=t_all[:, j0:j1, :], in1=e_all[:, j0:j1, :], op=ALU.max)
+                nc.sync.dma_start(out=out_view[:, j0:j1, :], in_=t_all[:, j0:j1, :])
+
+        ctx.enter_context(tc.manual_schedule())
+        by_unit = {"T": T_, "P1": P1_, "EX": EX_, "RC": RC_, "ST": ST_, "W": W_, "CP": CP_, "Q": Q_, "F": F_, "Z": Z_}
+        by_tile = {"QZ": QZ_, "O": O_, "TB": TB_, "CL": CL_, "E": E_}
+        for k in range(-6, UNITS + 30):
+            for at_step, kind, a in FEAT:
+                if at_step == k:
+                    if kind == "W":
+                        feat_widen(a)
+                    else:
+                        feat_quantise(a)
+            for stage, lag in ORDER:
+                u = k - lag
+                if stage == "SQ":
+                    if k >= -1:
+                        squares_next(SQ_PACE[0] if k < SQ_PACE[1] else SQ_PACE[2])
+                elif 0 <= u < UNITS:
+                    if stage in by_unit:
+                        by_unit[stage](u)
+                    elif u % PLANES == PLANES - 1:
+                        by_tile[stage](u // PLANES)
+        finish(LN_EARLY)
+        logs(LN_LATE)
+        finish(LN_LATE)

@@ -27,29 +27,31 @@ ACT = mybir.ActivationFunctionType
 
 BLOCKS = ((0, 256), (256, 256), (512, 256), (768, 256))
 ORDER = (
-    ("CP", 6),
-    ("F", 8),
+    ("Q", 7),
+    ("QZ", 9),
     ("EX", 2),
+    ("TB", 10),
+    ("CL", 10),
+    ("F", 8),
     ("ST", 5),
-    ("CL", 14),
+    ("CP", 6),
+    ("E", 18),
     ("O", 9),
-    ("P1", 0),
-    ("W", 5),
-    ("E", 15),
-    ("Z", 8),
-    ("TB", 9),
-    ("Q", 6),
-    ("RC", 2),
     ("SQ", 0),
-    ("QZ", 8),
+    ("P1", 0),
+    ("RC", 2),
+    ("Z", 8),
+    ("W", 5),
     ("T", -1),
 )
-FEAT = ((-5, "W", 2), (2, "W", 1), (3, "W", 0), (7, "Q", 0), (7, "Q", 1), (8, "Q", 2))
-CP_ON_VECTOR = (0, 1, 22, 23)
-C0_ON_SCALAR = (4, 5, 6)
+SQ_ON_VECTOR = ((0, 2),)
+FEAT = ((5, "W", 2), (4, "G", 0), (10, "Q", 2), (7, "Q", 1), (2, "W", 0), (1, "W", 1), (8, "Q", 0))
+CP_ON_VECTOR = tuple(range(8)) + (22, 23)
+C0_ON_SCALAR = tuple(range(7))
+CL_ON_VECTOR = (7,)
 LN_EARLY = ((0, 2), (2, 4), (4, 6))
 LN_LATE = ((6, 7), (7, 8))
-SQ_PACE = (2, 6, 4)
+SQ_PACE = 3
 
 
 def tile_kplanesgaussiananchordecoder_d2p_kernel(
@@ -63,7 +65,8 @@ def tile_kplanesgaussiananchordecoder_d2p_kernel(
         work = ctx.enter_context(tc.tile_pool(name="work", bufs=4))
         psum = ctx.enter_context(tc.psum_pool(name="psum", bufs=2))
 
-        ptsb = keep.tile([P, N, 3], BF16, name="ptsb")
+        ptsl = keep.tile([P, T, 3], BF16, name="ptsl")
+        ptsb = keep.tile([P, N // 2, 3], BF16, name="ptsb")
         cenb = keep.tile([P, PLANES, 2 * T], BF16, name="cenb")
         gab = keep.tile([P, PLANES, M], BF16, name="gab")
         b1b = keep.tile([P, H], BF16, name="b1b")
@@ -73,28 +76,23 @@ def tile_kplanesgaussiananchordecoder_d2p_kernel(
         w1s = keep.tile([P, H], U8, name="w1s", align_bytes=64)
         fbytes = [keep.tile([P, T, C], U8, name="fbytes%d" % a) for a in range(PLANES)]
 
-        flat = pts.rearrange("n x -> (n x)")
-        n_first = BLOCKS[0][1]
+        half = N // 2
         nc.scalar.dma_start(out=cenb[:], in_=cen.rearrange("a (p k) e -> p a (k e)", k=T))
-        nc.sync.dma_start(
-            out=ptsb[:, 0:n_first, :].rearrange("p n x -> p (n x)"),
-            in_=flat[0 : 3 * n_first].partition_broadcast(P),
-        )
+        nc.sync.dma_start(out=ptsl[:], in_=pts[0:half, :].rearrange("(p k) x -> p k x", k=T))
         nc.sync.dma_start(out=fbytes[0][:], in_=feat_bytes[0].rearrange("(p t) c -> p t c", t=T))
         for i in range(4):
             nc.sync.dma_start(
                 out=fscale[32 * i : 32 * i + 32, :, :],
                 in_=feat_scale.rearrange("a i j -> i a j")[i].partition_broadcast(32),
             )
-        nc.sync.dma_start(
-            out=ptsb[:, n_first:N, :].rearrange("p n x -> p (n x)"),
-            in_=flat[3 * n_first : 3 * N].partition_broadcast(P),
-        )
         nc.sync.dma_start(out=gab[:].rearrange("p a m -> p (a m)"), in_=ga.rearrange("a m -> (a m)").partition_broadcast(P))
         for a in (1, 2):
             nc.sync.dma_start(out=fbytes[a][:], in_=feat_bytes[a].rearrange("(p t) c -> p t c", t=T))
+        nc.sync.dma_start(
+            out=ptsb[:].rearrange("p n x -> p (n x)"),
+            in_=pts.rearrange("n x -> (n x)")[3 * half : 3 * N].partition_broadcast(P),
+        )
         nc.sync.dma_start(out=gcb[:], in_=gc.rearrange("(p t) -> p t", t=T))
-        nc.sync.dma_start(out=b1b[:], in_=b1.partition_broadcast(P))
         nc.sync.dma_start(out=w1w[:].bitcast(I32), in_=w1_words[0].bitcast(I32))
         nc.gpsimd.memset(w1s[:].bitcast(I32), 0)
         for q in range(4):
@@ -102,6 +100,10 @@ def tile_kplanesgaussiananchordecoder_d2p_kernel(
                 out=w1s[32 * q : 32 * q + 4, :].bitcast(I32), in_=w1_scales[0][4 * q : 4 * q + 4, :].bitcast(I32)
             )
 
+        nc.sync.dma_start(out=b1b[:], in_=b1.partition_broadcast(P))
+
+        identb = keep.tile([P, P], BF16, name="identb")
+        make_identity(nc, identb[:])
         ident = keep.tile([P, P], F32, name="ident")
         make_identity(nc, ident[:])
         cen32 = keep.tile([P, PLANES, 2 * T], F32, name="cen32")
@@ -113,7 +115,6 @@ def tile_kplanesgaussiananchordecoder_d2p_kernel(
         t_all = keep.tile([P, NT, H], F32, name="t_all")
         e_all = keep.tile([P, NT, H], F32, name="e_all")
 
-        nc.gpsimd.tensor_copy(out=gc32[:], in_=gcb[:])
         sqs, d2s, xs, mns, exs, sms, rss, abs_, ats, grs, cos, fs, gs = {}, {}, {}, {}, {}, {}, {}, {}, {}, {}, {}, {}, {}
         zcs, os_, lows, fgs = {}, {}, {}, {}
 
@@ -134,10 +135,6 @@ def tile_kplanesgaussiananchordecoder_d2p_kernel(
                     op0=ALU.mult,
                     op1=ALU.add,
                 )
-            nc.gpsimd.tensor_copy(
-                out=gar[:, a, :].rearrange("p (u q e) -> p u q e", u=2, e=2),
-                in_=gab[:, a, :].rearrange("p (q u e) -> p u q e", u=2, e=2),
-            )
             fgs[a] = fgrouped
 
         def feat_quantise(a):
@@ -145,7 +142,38 @@ def tile_kplanesgaussiananchordecoder_d2p_kernel(
                 out=fcodes[a][:].bitcast(FP8X4), scales=fplane[a][:], in_=fgs[a][:].rearrange("p s c t -> p (s c t)")
             )
 
-        pieces = [(b, a, t, e) for b in range(len(BLOCKS)) for a in range(PLANES) for t in range(T) for e in range(2)]
+        def gains():
+            for a in range(PLANES):
+                nc.vector.tensor_copy(
+                    out=gar[:, a, :].bitcast(F32).rearrange("p (u q) -> p u q", u=2),
+                    in_=gab[:, a, :].bitcast(F32).rearrange("p (q u) -> p u q", u=2),
+                )
+            nc.vector.tensor_copy(out=gc32[:], in_=gcb[:])
+
+        us = {}
+
+        def spread(b):
+            ua = psum.tile([P, 2, 2 * P], F32, name="ua", tag="f", bufs=3)
+            if b == 0:
+                ub = psum.tile([P, 2 * P], F32, name="ub", tag="f", bufs=3)
+            else:
+                ub = psum.tile([P, 2 * P], F32, name="ub", tag="o", bufs=1)
+            for c in range(3):
+                us[(b, c)] = ua[:, c, :] if c < 2 else ub[:]
+                for k in range(2):
+                    nc.tensor.matmul(
+                        out=us[(b, c)][:, P * k : P * k + P],
+                        lhsT=ptsl[:, 2 * b + k, c : c + 1].to_broadcast([P, P]),
+                        rhs=identb[:],
+                        start=True,
+                        stop=True,
+                    )
+
+        def points(b, c):
+            n0, width = BLOCKS[b]
+            return us[(b, c)] if b < 2 else ptsb[:, n0 - half : n0 - half + width, c]
+
+        pieces = [(b, a, t, e) for b in range(len(BLOCKS)) for a in range(PLANES) for t in range(T) for e in range(2) if (b, a) not in SQ_ON_VECTOR]
 
         def square(b, a, t, e):
             n0, width = BLOCKS[b]
@@ -154,27 +182,44 @@ def tile_kplanesgaussiananchordecoder_d2p_kernel(
                 sqs[(b, a)] = sq
             nc.scalar.activation(
                 out=sqs[(b, a)][:, t, e, :],
-                in_=ptsb[:, n0 : n0 + width, COORDS[a][e]],
+                in_=points(b, COORDS[a][e]),
                 func=ACT.Square,
                 bias=cen32[:, a, 2 * t + e : 2 * t + e + 1],
                 scale=-1.0,
             )
 
+        def squares_on_vector(b, a):
+            n0, width = BLOCKS[b]
+            sq = sqp.tile([P, T, 2, width], F32, name="sq")
+            sqs[(b, a)] = sq
+            for t in range(T):
+                for e in range(2):
+                    diff = work.tile([P, width], F32, name="diff")
+                    nc.vector.tensor_scalar(
+                        out=diff[:],
+                        in0=points(b, COORDS[a][e]),
+                        scalar1=cen32[:, a, 2 * t + e : 2 * t + e + 1],
+                        scalar2=None,
+                        op0=ALU.subtract,
+                    )
+                    nc.vector.tensor_tensor(out=sq[:, t, e, :], in0=diff[:], in1=diff[:], op=ALU.mult)
+
         def block_of(j):
             return [b for b, (n0, width) in enumerate(BLOCKS) if n0 <= P * j < n0 + width][0]
 
-        def squares_until(count):
-            while len(pieces) > len(BLOCKS) * 24 - count:
-                square(*pieces[0])
-                pieces.remove(pieces[0])
-
         def squares_next(count):
-            squares_until(min(len(BLOCKS) * 24, len(BLOCKS) * 24 - len(pieces) + count))
+            for piece in pieces[:count]:
+                square(*piece)
+                pieces.remove(piece)
+
+        def squares_for(b, a):
+            while pieces and pieces[0][:2] <= (b, a):
+                squares_next(1)
 
         def T_(u):
             j, a = divmod(u, PLANES)
             b = block_of(j)
-            squares_until(24 * b + 8 * a + 8)
+            squares_for(b, a)
             col0 = P * j - BLOCKS[b][0]
             d2 = psum.tile([P, M], F32, name="d2", bufs=2)
             for t in range(T):
@@ -321,7 +366,8 @@ def tile_kplanesgaussiananchordecoder_d2p_kernel(
 
         def CL_(j):
             low = work.tile([P, H], F32, name="low")
-            nc.gpsimd.tensor_scalar(
+            engine = nc.vector if j in CL_ON_VECTOR else nc.gpsimd
+            engine.tensor_scalar(
                 out=low[:], in0=t_all[:, j, :], scalar1=40.0, scalar2=-100.0, op0=ALU.min, op1=ALU.max
             )
             lows[j] = low
@@ -335,28 +381,30 @@ def tile_kplanesgaussiananchordecoder_d2p_kernel(
             for j0, j1 in groups:
                 nc.scalar.activation(out=e_all[:, j0:j1, :], in_=e_all[:, j0:j1, :], func=ACT.Ln, bias=1.0)
 
-        out_view = out.rearrange("(j n) h -> n j h", n=P)
+        out_low = out[0:half, :].rearrange("(r k) h -> r k h", k=T)
+        out_high = out[half:N, :].rearrange("(j r) h -> r j h", r=P)
 
         def finish(groups):
             for j0, j1 in groups:
                 nc.vector.tensor_tensor(out=t_all[:, j0:j1, :], in0=t_all[:, j0:j1, :], in1=e_all[:, j0:j1, :], op=ALU.max)
-                nc.sync.dma_start(out=out_view[:, j0:j1, :], in_=t_all[:, j0:j1, :])
+                rows = out_low[:, j0:j1, :] if j1 <= T else out_high[:, j0 - T : j1 - T, :]
+                nc.sync.dma_start(out=rows, in_=t_all[:, j0:j1, :])
 
         ctx.enter_context(tc.manual_schedule())
+        spread(0)
+        spread(1)
+        squares_on_vector(0, 2)
         by_unit = {"T": T_, "P1": P1_, "EX": EX_, "RC": RC_, "ST": ST_, "W": W_, "CP": CP_, "Q": Q_, "F": F_, "Z": Z_}
         by_tile = {"QZ": QZ_, "O": O_, "TB": TB_, "CL": CL_, "E": E_}
         for k in range(-6, UNITS + 30):
             for at_step, kind, a in FEAT:
                 if at_step == k:
-                    if kind == "W":
-                        feat_widen(a)
-                    else:
-                        feat_quantise(a)
+                    {"W": feat_widen, "Q": feat_quantise, "G": lambda i: gains()}[kind](a)
             for stage, lag in ORDER:
                 u = k - lag
                 if stage == "SQ":
                     if k >= -1:
-                        squares_next(SQ_PACE[0] if k < SQ_PACE[1] else SQ_PACE[2])
+                        squares_next(SQ_PACE)
                 elif 0 <= u < UNITS:
                     if stage in by_unit:
                         by_unit[stage](u)

from contextlib import ExitStack

import concourse.mybir as mybir
from concourse.masks import make_identity

N, PLANES, M, C, H = 1024, 3, 512, 512, 512
INV_WIDTH2 = 1.0 / 0.0018
COORDS = ((0, 1), (0, 2), (1, 2))

P = 128
T = 4
NT = N // P
UNITS = NT * PLANES

FLOPS = 2 * N * M * C * PLANES + 2 * N * C * H

F32 = mybir.dt.float32
BF16 = mybir.dt.bfloat16
U32 = mybir.dt.uint32
I32 = mybir.dt.int32
U8 = mybir.dt.uint8
FP8 = mybir.dt.float8_e4m3fn
FP8X4 = mybir.dt.float8_e4m3fn_x4
FP4X4 = mybir.dt.float4_e2m1fn_x4
ALU = mybir.AluOpType
ACT = mybir.ActivationFunctionType

BLOCKS = ((0, 256), (256, 256), (512, 256), (768, 256))
ORDER = (
    ("Q", 7),
    ("QZ", 9),
    ("EX", 2),
    ("TB", 10),
    ("CL", 10),
    ("F", 8),
    ("ST", 5),
    ("CP", 6),
    ("E", 18),
    ("O", 9),
    ("SQ", 0),
    ("P1", 0),
    ("RC", 2),
    ("Z", 8),
    ("W", 5),
    ("T", -1),
)
SQ_ON_VECTOR = ((0, 2),)
FEAT = ((5, "W", 2), (4, "G", 0), (10, "Q", 2), (7, "Q", 1), (2, "W", 0), (1, "W", 1), (8, "Q", 0))
CP_ON_VECTOR = tuple(range(8)) + (22, 23)
C0_ON_SCALAR = tuple(range(7))
CL_ON_VECTOR = (7,)
LN_EARLY = ((0, 2), (2, 4), (4, 6))
LN_LATE = ((6, 7), (7, 8))
SQ_PACE = 3


def tile_kplanesgaussiananchordecoder_d2p_kernel(
    tc, pts, cen, ga, feat_bytes, feat_scale, gc, w1_words, w1_scales, b1, out
):
    nc = tc.nc
    with ExitStack() as ctx:
        keep = ctx.enter_context(tc.tile_pool(name="keep", bufs=1))
        prep = ctx.enter_context(tc.tile_pool(name="prep", bufs=3))
        sqp = ctx.enter_context(tc.tile_pool(name="sqp", bufs=5))
        work = ctx.enter_context(tc.tile_pool(name="work", bufs=4))
        psum = ctx.enter_context(tc.psum_pool(name="psum", bufs=2))

        ptsl = keep.tile([P, T, 3], BF16, name="ptsl")
        ptsb = keep.tile([P, N // 2, 3], BF16, name="ptsb")
        cenb = keep.tile([P, PLANES, 2 * T], BF16, name="cenb")
        gab = keep.tile([P, PLANES, M], BF16, name="gab")
        b1b = keep.tile([P, H], BF16, name="b1b")
        gcb = keep.tile([P, T], BF16, name="gcb")
        fscale = keep.tile([P, PLANES, 4], F32, name="fscale")
        w1w = keep.tile([P, 2 * H], U8, name="w1w", align_bytes=64)
        w1s = keep.tile([P, H], U8, name="w1s", align_bytes=64)
        fbytes = [keep.tile([P, T, C], U8, name="fbytes%d" % a) for a in range(PLANES)]

        half = N // 2
        nc.scalar.dma_start(out=cenb[:], in_=cen.rearrange("a (p k) e -> p a (k e)", k=T))
        nc.sync.dma_start(out=ptsl[:], in_=pts[0:half, :].rearrange("(p k) x -> p k x", k=T))
        nc.sync.dma_start(out=fbytes[0][:], in_=feat_bytes[0].rearrange("(p t) c -> p t c", t=T))
        for i in range(4):
            nc.sync.dma_start(
                out=fscale[32 * i : 32 * i + 32, :, :],
                in_=feat_scale.rearrange("a i j -> i a j")[i].partition_broadcast(32),
            )
        nc.sync.dma_start(out=gab[:].rearrange("p a m -> p (a m)"), in_=ga.rearrange("a m -> (a m)").partition_broadcast(P))
        for a in (1, 2):
            nc.sync.dma_start(out=fbytes[a][:], in_=feat_bytes[a].rearrange("(p t) c -> p t c", t=T))
        nc.sync.dma_start(
            out=ptsb[:].rearrange("p n x -> p (n x)"),
            in_=pts.rearrange("n x -> (n x)")[3 * half : 3 * N].partition_broadcast(P),
        )
        nc.sync.dma_start(out=gcb[:], in_=gc.rearrange("(p t) -> p t", t=T))
        nc.sync.dma_start(out=w1w[:].bitcast(I32), in_=w1_words[0].bitcast(I32))
        nc.gpsimd.memset(w1s[:].bitcast(I32), 0)
        for q in range(4):
            nc.sync.dma_start(
                out=w1s[32 * q : 32 * q + 4, :].bitcast(I32), in_=w1_scales[0][4 * q : 4 * q + 4, :].bitcast(I32)
            )

        nc.sync.dma_start(out=b1b[:], in_=b1.partition_broadcast(P))

        identb = keep.tile([P, P], BF16, name="identb")
        make_identity(nc, identb[:])
        ident = keep.tile([P, P], F32, name="ident")
        make_identity(nc, ident[:])
        cen32 = keep.tile([P, PLANES, 2 * T], F32, name="cen32")
        nc.vector.tensor_copy(out=cen32[:], in_=cenb[:])
        gc32 = keep.tile([P, T], F32, name="gc32")
        gar = keep.tile([P, PLANES, M], BF16, name="gar")
        fcodes = [keep.tile([P, C], U32, name="fcodes%d" % a, align_bytes=64) for a in range(PLANES)]
        fplane = [keep.tile([P, C], U8, name="fplane%d" % a, align_bytes=64) for a in range(PLANES)]
        t_all = keep.tile([P, NT, H], F32, name="t_all")
        e_all = keep.tile([P, NT, H], F32, name="e_all")

        sqs, d2s, xs, mns, exs, sms, rss, abs_, ats, grs, cos, fs, gs = {}, {}, {}, {}, {}, {}, {}, {}, {}, {}, {}, {}, {}
        zcs, os_, lows, fgs = {}, {}, {}, {}

        def feat_widen(a):
            wide = prep.tile([P, T, C], BF16, name="wide")
            nc.vector.tensor_copy(
                out=wide[:].rearrange("p t c -> p (t c)"),
                in_=fbytes[a][:].rearrange("p t c -> p (t c)").bitcast(FP8),
            )
            fgrouped = prep.tile([P, T, P, T], BF16, name="fgrouped", align_bytes=64)
            for j in range(4):
                cols = slice(32 * j, 32 * j + 32)
                nc.gpsimd.tensor_scalar(
                    out=fgrouped[:, :, cols, :],
                    in0=wide[:, :, 128 * j : 128 * j + 128].rearrange("p t (c s) -> p s c t", s=T),
                    scalar1=fscale[:, a, j : j + 1],
                    scalar2=0.0,
                    op0=ALU.mult,
                    op1=ALU.add,
                )
            fgs[a] = fgrouped

        def feat_quantise(a):
            nc.vector.quantize_mx(
                out=fcodes[a][:].bitcast(FP8X4), scales=fplane[a][:], in_=fgs[a][:].rearrange("p s c t -> p (s c t)")
            )

        def gains():
            for a in range(PLANES):
                nc.vector.tensor_copy(
                    out=gar[:, a, :].bitcast(F32).rearrange("p (u q) -> p u q", u=2),
                    in_=gab[:, a, :].bitcast(F32).rearrange("p (q u) -> p u q", u=2),
                )
            nc.vector.tensor_copy(out=gc32[:], in_=gcb[:])

        us = {}

        def spread(b):
            ua = psum.tile([P, 2, 2 * P], F32, name="ua", tag="f", bufs=3)
            if b == 0:
                ub = psum.tile([P, 2 * P], F32, name="ub", tag="f", bufs=3)
            else:
                ub = psum.tile([P, 2 * P], F32, name="ub", tag="o", bufs=1)
            for c in range(3):
                us[(b, c)] = ua[:, c, :] if c < 2 else ub[:]
                for k in range(2):
                    nc.tensor.matmul(
                        out=us[(b, c)][:, P * k : P * k + P],
                        lhsT=ptsl[:, 2 * b + k, c : c + 1].to_broadcast([P, P]),
                        rhs=identb[:],
                        start=True,
                        stop=True,
                    )

        def points(b, c):
            n0, width = BLOCKS[b]
            return us[(b, c)] if b < 2 else ptsb[:, n0 - half : n0 - half + width, c]

        pieces = [(b, a, t, e) for b in range(len(BLOCKS)) for a in range(PLANES) for t in range(T) for e in range(2) if (b, a) not in SQ_ON_VECTOR]

        def square(b, a, t, e):
            n0, width = BLOCKS[b]
            if (b, a) not in sqs:
                sq = sqp.tile([P, T, 2, width], F32, name="sq")
                sqs[(b, a)] = sq
            nc.scalar.activation(
                out=sqs[(b, a)][:, t, e, :],
                in_=points(b, COORDS[a][e]),
                func=ACT.Square,
                bias=cen32[:, a, 2 * t + e : 2 * t + e + 1],
                scale=-1.0,
            )

        def squares_on_vector(b, a):
            n0, width = BLOCKS[b]
            sq = sqp.tile([P, T, 2, width], F32, name="sq")
            sqs[(b, a)] = sq
            for t in range(T):
                for e in range(2):
                    diff = work.tile([P, width], F32, name="diff")
                    nc.vector.tensor_scalar(
                        out=diff[:],
                        in0=points(b, COORDS[a][e]),
                        scalar1=cen32[:, a, 2 * t + e : 2 * t + e + 1],
                        scalar2=None,
                        op0=ALU.subtract,
                    )
                    nc.vector.tensor_tensor(out=sq[:, t, e, :], in0=diff[:], in1=diff[:], op=ALU.mult)

        def block_of(j):
            return [b for b, (n0, width) in enumerate(BLOCKS) if n0 <= P * j < n0 + width][0]

        def squares_next(count):
            for piece in pieces[:count]:
                square(*piece)
                pieces.remove(piece)

        def squares_for(b, a):
            while pieces and pieces[0][:2] <= (b, a):
                squares_next(1)

        def T_(u):
            j, a = divmod(u, PLANES)
            b = block_of(j)
            squares_for(b, a)
            col0 = P * j - BLOCKS[b][0]
            d2 = psum.tile([P, M], F32, name="d2", bufs=2)
            for t in range(T):
                pos = (t % 2) * 256 + (t // 2) * 128
                for e in range(2):
                    nc.tensor.matmul(
                        out=d2[:, pos : pos + P],
                        lhsT=sqs[(b, a)][:, t, e, col0 : col0 + P],
                        rhs=ident[:],
                        start=(e == 0),
                        stop=(e == 1),
                        is_transpose=True,
                    )
            d2s[u] = d2

        def P1_(u):
            j, a = divmod(u, PLANES)
            x = work.tile([P, M], F32, name="x")
            mn = work.tile([P, 1], F32, name="mn")
            nc.vector.tensor_scalar(
                out=x[:], in0=d2s[u][:], scalar1=INV_WIDTH2, scalar2=None, op0=ALU.mult, op1=ALU.min, accum_out=mn[:]
            )
            xs[u], mns[u] = x, mn

        def EX_(u):
            j, a = divmod(u, PLANES)
            if a == 0:
                sm = work.tile([P, PLANES], F32, name="sm")
                sms[j] = sm
            ex = work.tile([P, M], F32, name="ex", bufs=8)
            nc.scalar.activation(
                out=ex[:].rearrange("n (w e) -> n w e", e=2),
                in_=xs[u][:].rearrange("n (e w) -> n w e", e=2),
                func=ACT.Exp,
                bias=mns[u][:],
                scale=-1.0,
                accum_out=sms[j][:, a : a + 1],
            )
            exs[u] = ex

        def RC_(u):
            j, a = divmod(u, PLANES)
            if a == PLANES - 1:
                rs = work.tile([P, PLANES], F32, name="rs")
                nc.vector.reciprocal(out=rs[:], in_=sms[j][:])
                rss[j] = rs

        def ST_(u):
            j, a = divmod(u, PLANES)
            ab = work.tile([P, M], BF16, name="ab")
            nc.vector.scalar_tensor_tensor(
                out=ab[:], in0=exs[u][:], scalar=rss[j][:, a : a + 1], in1=gar[:, a, :], op0=ALU.mult, op1=ALU.mult
            )
            abs_[u] = ab

        def W_(u):
            at = psum.tile([P, 2, P], F32, name="at", bufs=2)
            words = abs_[u][:].bitcast(F32)
            for i in range(2):
                nc.tensor.transpose(at[:, i, :], words[:, P * i : P * i + P], ident[:])
            ats[u] = at

        def CP_(u):
            grouped = work.tile([P, P, T], BF16, name="grouped", align_bytes=64)
            copy = nc.vector.tensor_copy if u in CP_ON_VECTOR else nc.scalar.copy
            copy(
                out=grouped[:].rearrange("p n t -> p (n t)").bitcast(F32).rearrange("p (n u) -> p n u", u=2),
                in_=ats[u][:].rearrange("p u n -> p n u"),
            )
            grs[u] = grouped

        def Q_(u):
            codes = work.tile([P, P], U32, name="codes", bufs=6, align_bytes=64)
            plane = work.tile([P, P], U8, name="plane", bufs=6, align_bytes=64)
            nc.vector.quantize_mx(
                out=codes[:].bitcast(FP8X4), scales=plane[:], in_=grs[u][:].rearrange("p n t -> p (n t)")
            )
            cos[u] = (codes, plane)

        def F_(u):
            j, a = divmod(u, PLANES)
            f = psum.tile([P, T, P], F32, name="f", bufs=3)
            codes, plane = cos[u]
            for s in range(T):
                cols = slice(P * s, P * s + P)
                nc.tensor.matmul_mx(
                    out=f[:, s, :],
                    lhsT=fcodes[a][:, cols].bitcast(FP8X4),
                    lhsT_scale=fplane[a][:, cols],
                    rhs=codes[:].bitcast(FP8X4),
                    rhs_scale=plane[:],
                    start=True,
                    stop=True,
                )
            fs[u] = f

        def Z_(u):
            j, a = divmod(u, PLANES)
            if a < PLANES - 1:
                g = work.tile([P, T, P], F32, name="g")
                if a == 0 and j in C0_ON_SCALAR:
                    for s in range(T):
                        nc.scalar.activation(out=g[:, s, :], in_=fs[u][:, s, :], func=ACT.Copy, scale=gc32[:, s : s + 1])
                elif a == 0:
                    nc.vector.tensor_tensor(
                        out=g[:], in0=fs[u][:], in1=gc32[:].unsqueeze(2).to_broadcast([P, T, P]), op=ALU.mult
                    )
                else:
                    nc.vector.tensor_tensor(out=g[:], in0=fs[u][:], in1=gs[u - 1][:], op=ALU.mult)
            else:
                g = work.tile([P, P, T], BF16, name="z", align_bytes=64)
                nc.vector.tensor_tensor(
                    out=g[:],
                    in0=fs[u][:].rearrange("p s n -> p n s"),
                    in1=gs[u - 1][:].rearrange("p s n -> p n s"),
                    op=ALU.mult,
                )
            gs[u] = g

        def QZ_(j):
            zcodes = work.tile([P, P], U32, name="zcodes", align_bytes=64)
            zplane = work.tile([P, P], U8, name="zplane", align_bytes=64)
            nc.vector.quantize_mx(
                out=zcodes[:].bitcast(FP8X4), scales=zplane[:], in_=gs[3 * j + 2][:].rearrange("p n t -> p (n t)")
            )
            zcs[j] = (zcodes, zplane)

        def O_(j):
            o = psum.tile([P, H], F32, name="o", bufs=1)
            zcodes, zplane = zcs[j]
            nc.tensor.matmul_mx(
                out=o[:],
                lhsT=zcodes[:].bitcast(FP8X4),
                lhsT_scale=zplane[:],
                rhs=w1w[:].bitcast(FP4X4),
                rhs_scale=w1s[:],
                start=True,
                stop=True,
            )
            os_[j] = o

        def TB_(j):
            nc.vector.tensor_tensor(out=t_all[:, j, :], in0=os_[j][:], in1=b1b[:], op=ALU.add)

        def CL_(j):
            low = work.tile([P, H], F32, name="low")
            engine = nc.vector if j in CL_ON_VECTOR else nc.gpsimd
            engine.tensor_scalar(
                out=low[:], in0=t_all[:, j, :], scalar1=40.0, scalar2=-100.0, op0=ALU.min, op1=ALU.max
            )
            lows[j] = low

        def E_(j):
            nc.scalar.activation(out=e_all[:, j, :], in_=lows[j][:], func=ACT.Exp)
            if j == LN_EARLY[-1][1] - 1:
                logs(LN_EARLY)

        def logs(groups):
            for j0, j1 in groups:
                nc.scalar.activation(out=e_all[:, j0:j1, :], in_=e_all[:, j0:j1, :], func=ACT.Ln, bias=1.0)

        out_low = out[0:half, :].rearrange("(r k) h -> r k h", k=T)
        out_high = out[half:N, :].rearrange("(j r) h -> r j h", r=P)

        def finish(groups):
            for j0, j1 in groups:
                nc.vector.tensor_tensor(out=t_all[:, j0:j1, :], in0=t_all[:, j0:j1, :], in1=e_all[:, j0:j1, :], op=ALU.max)
                rows = out_low[:, j0:j1, :] if j1 <= T else out_high[:, j0 - T : j1 - T, :]
                nc.sync.dma_start(out=rows, in_=t_all[:, j0:j1, :])

        ctx.enter_context(tc.manual_schedule())
        spread(0)
        spread(1)
        squares_on_vector(0, 2)
        by_unit = {"T": T_, "P1": P1_, "EX": EX_, "RC": RC_, "ST": ST_, "W": W_, "CP": CP_, "Q": Q_, "F": F_, "Z": Z_}
        by_tile = {"QZ": QZ_, "O": O_, "TB": TB_, "CL": CL_, "E": E_}
        for k in range(-6, UNITS + 30):
            for at_step, kind, a in FEAT:
                if at_step == k:
                    {"W": feat_widen, "Q": feat_quantise, "G": lambda i: gains()}[kind](a)
            for stage, lag in ORDER:
                u = k - lag
                if stage == "SQ":
                    if k >= -1:
                        squares_next(SQ_PACE)
                elif 0 <= u < UNITS:
                    if stage in by_unit:
                        by_unit[stage](u)
                    elif u % PLANES == PLANES - 1:
                        by_tile[stage](u // PLANES)
        finish(LN_EARLY)
        logs(LN_LATE)
        finish(LN_LATE)
